import numpy as np
import ml_dtypes


def mxq(x, axis, fmt="e4m3"):
    dtype, down = {"e4m3": (ml_dtypes.float8_e4m3fn, 7), "e5m2": (ml_dtypes.float8_e5m2, 14)}[fmt]
    v = np.moveaxis(np.asarray(x, np.float32).astype(ml_dtypes.bfloat16).astype(np.float64), axis, -1)
    blocks = v.reshape(v.shape[:-1] + (-1, 32))
    amax = np.abs(blocks).max(-1, keepdims=True)
    byte = np.maximum(np.where(amax > 0, np.frexp(amax)[1] - 1 + 127, 0) - down, 1)
    scale = np.exp2(byte - 127.0)
    codes = (blocks / scale).astype(np.float32).astype(dtype).astype(np.float64)
    return np.moveaxis((codes * scale).reshape(v.shape), -1, axis)


WIDE = False


def mx_kscale(k):
    if not WIDE:
        return np.ones(k)
    levels = np.array([10, -10, 5, -5, 0])
    if k % 512:
        return np.exp2(np.random.permutation(np.resize(levels, k // 32))).repeat(32)
    a = np.empty((k // 512, 16))
    for p in range(k // 512):
        a[p, :8] = np.random.permutation(np.resize(levels, 8))
        for g in range(8):
            far = levels[np.abs(levels - a[p, g]) >= 10]
            a[p, g + 8] = far[np.random.randint(len(far))]
    return np.exp2(a.ravel()).repeat(32)


def f64(x):
    return np.asarray(x).astype(np.float64)


def striped(idx):
    return np.tile(idx.reshape(-1, 16).T, (8, 1)).astype(np.uint16)


def unstriped(offs):
    return offs[:16].T.reshape(-1).astype(np.int64)


def silu(v):
    return v / (1.0 + np.exp(-np.maximum(v, -700.0)))


K, T, E, C, H, N = 512, 512, 8, 128, 512, 512


def by_expert(wq, xq):
    return np.concatenate([wq[e].T @ xq[:, e * C:(e + 1) * C] for e in range(E)], axis=1)


def setup_inputs():
    n = np.random.standard_normal
    s = mx_kscale(K)[:, None]
    u = mx_kscale(H)
    first = np.random.permutation(np.repeat(np.arange(E), T // E))
    second = (first + 1 + np.random.permutation(np.repeat(np.arange(E - 1), -(-T // (E - 1)))[:T])) % E
    while np.bincount(second, minlength=E).max() != T // E:
        load = np.bincount(second, minlength=E); hi, lo = int(load.argmax()), int(load.argmin())
        t = np.flatnonzero((second == hi) & (first != lo))[0]; second[t] = lo
    slot_token = np.empty(E * C, np.int64); pos = np.empty((2, T), np.int64); fill = np.zeros(E, np.int64)
    place = np.stack([np.random.permutation(C) for _ in range(E)])
    for r, deal in enumerate((first, second)):
        for t in np.random.permutation(T):
            e = deal[t]; j = e * C + place[e, fill[e]]; fill[e] += 1; slot_token[j] = t; pos[r, t] = j
    g = np.random.uniform(0.2, 0.8, T)
    return {
        "xT": (n((K, T)) * s).astype(np.float32),
        "w1": (n((E, K, H)) / np.sqrt(K) / s[None] * u[None, None, :]).astype(np.float32),
        "w2": (n((E, H, N)) / np.sqrt(H) / u[None, :, None]).astype(np.float32),
        "gate": np.stack([np.tile(g, (N, 1)), np.tile(1.0 - g, (N, 1))]).astype(np.float32),
        "offs": striped(slot_token),
        "pos1": striped(pos[0]),
        "pos2": striped(pos[1]),
    }


def reference(xT, w1, w2, gate, offs, pos1, pos2):
    idx = unstriped(offs)
    xq = mxq(f64(xT)[:, idx], 0, "e4m3")
    h = silu(by_expert(mxq(f64(w1), 1, "e4m3"), xq))
    y = by_expert(mxq(f64(w2), 1, "e4m3"), mxq(h, 0, "e4m3"))
    return f64(gate[0]) * y[:, unstriped(pos1)] + f64(gate[1]) * y[:, unstriped(pos2)]

@@ -1,0 +1,244 @@
+from contextlib import ExitStack
+
+import concourse.mybir as mybir
+from concourse.masks import make_identity
+
+K, T, E, C, H, N = 512, 512, 8, 128, 512, 512
+FLOPS = 2 * E * C * (K * H + H * N)
+
+F32 = mybir.dt.float32
+BF16 = mybir.dt.bfloat16
+U32 = mybir.dt.uint32
+U16 = mybir.dt.uint16
+U8 = mybir.dt.uint8
+FP8X4 = mybir.dt.float8_e4m3fn_x4
+SILU = mybir.ActivationFunctionType.Silu
+MULT = mybir.AluOpType.mult
+ADD = mybir.AluOpType.add
+
+P = 128
+PACK = 4
+NB = N // P
+RAW_BUFS = 14
+GATHER_CUTS = (0, 256, 640, 1024)
+GROUP = 4
+
+
+def tile_routed_moe_kernel(tc, xT, w1, w2, gate, offs, pos1, pos2, out):
+    nc = tc.nc
+    with ExitStack() as ctx:
+        lists = ctx.enter_context(tc.tile_pool(name="lists", bufs=1))
+        keep = ctx.enter_context(tc.tile_pool(name="keep", bufs=1))
+        raws = ctx.enter_context(tc.tile_pool(name="raws", bufs=RAW_BUFS))
+        stage = ctx.enter_context(tc.tile_pool(name="stage", bufs=5))
+        quant = ctx.enter_context(tc.tile_pool(name="quant", bufs=3))
+        comb = ctx.enter_context(tc.tile_pool(name="comb", bufs=3))
+        psum1 = ctx.enter_context(tc.psum_pool(name="psum1", bufs=2))
+        psum2 = ctx.enter_context(tc.psum_pool(name="psum2", bufs=1))
+        psum3 = ctx.enter_context(tc.psum_pool(name="psum3", bufs=2))
+
+        offs_t = lists.tile([P, E * C // 16], U16, name="offs_t")
+        nc.sync.dma_start(offs_t[:], offs)
+
+        x_raw = raws.tile([P, PACK, T], F32, tag="raw")
+        nc.sync.dma_start(out=x_raw[:], in_=xT.rearrange("(p j) t -> p j t", j=PACK))
+
+        def load_matrix(w, e):
+            raw = raws.tile([P, PACK, 512], F32, tag="raw")
+            nc.sync.dma_start(out=raw[:], in_=w[e].rearrange("(p j) c -> p j c", j=PACK))
+            return raw
+
+        order = [(1, 0)]
+        for e in range(E):
+            if e + 1 < E:
+                order.append((1, e + 1))
+            order.append((2, e))
+        raw_of = {}
+        for which, e in order:
+            raw_of[(which, e)] = load_matrix(w1 if which == 1 else w2, e)
+
+        pos1_t = lists.tile([P, T // 16], U16, name="pos1_t")
+        nc.sync.dma_start(pos1_t[:], pos1)
+        pos2_t = lists.tile([P, T // 16], U16, name="pos2_t")
+        nc.sync.dma_start(pos2_t[:], pos2)
+
+        gate_t = []
+        for nb in range(NB):
+            g = raws.tile([P, 2, T], F32, tag="raw", name="gate_t%d" % nb)
+            nc.sync.dma_start(out=g[:], in_=gate[:, nb * P:(nb + 1) * P, :].rearrange("r p t -> p r t"))
+            gate_t.append(g)
+
+        ident = keep.tile([P, P], F32, name="ident")
+        make_identity(nc, ident[:])
+
+        warm_in = keep.tile([P, 1], F32, name="warm_in")
+        warm_out = keep.tile([P, 1], F32, name="warm_out")
+        nc.gpsimd.memset(warm_in[:], 0.0)
+        nc.scalar.activation(out=warm_out[:], in_=warm_in[:], func=SILU)
+
+        x_codes = keep.tile([P, T], U32, name="x_codes", align_bytes=64)
+        x_scales = keep.tile([P, T], U8, name="x_scales", align_bytes=64)
+        nc.gpsimd.memset(x_scales[:], 0)
+        x_grouped = keep.tile([P, PACK * T], BF16, name="x_grouped", align_bytes=64)
+        slot_codes = keep.tile([P, E * C], U32, name="slot_codes", align_bytes=64)
+        slot_scales = keep.tile([P, E * C], U8, name="slot_scales", align_bytes=64)
+        y_sb = [keep.tile([P, E * C], F32, name="y_sb%d" % nb) for nb in range(NB)]
+
+        def plain_interleave(copy, grouped, raw, c0, c1):
+            copy(
+                out=grouped[:, PACK * c0:PACK * c1].rearrange("p (c i j) -> p c j i", i=4, j=PACK),
+                in_=raw[:, :, c0:c1].rearrange("p j (c i) -> p c j i", i=4),
+            )
+
+        def gather(s):
+            a, b = GATHER_CUTS[s], GATHER_CUTS[s + 1]
+            nc.vector.tensor_copy(slot_codes[:, a:b], x_codes[:].indirect(offs_t[:, a // 16:b // 16]))
+            nc.vector.tensor_copy(slot_scales[:, a:b], x_scales[:].indirect(offs_t[:, a // 16:b // 16]))
+
+        w1_grouped = {}
+        w1_q = {}
+        l1_acc = {}
+        h_q = {}
+        w2_grouped = {}
+        w2_q = {}
+        y_acc = {}
+
+        def stage_a(e, copy):
+            grouped = stage.tile([P, PACK * H], BF16, tag="grouped", align_bytes=64)
+            copy(
+                out=grouped[:].rearrange("p (t m j) -> p m j t", t=4, j=PACK),
+                in_=raw_of[(1, e)][:].rearrange("p j (m t) -> p m j t", t=4),
+            )
+            w1_grouped[e] = grouped
+
+        def stage_b(e):
+            codes = quant.tile([P, H], U32, tag="w1c", align_bytes=64)
+            scales = quant.tile([P, H], U8, tag="w1s", align_bytes=64)
+            nc.vector.quantize_mx(out=codes[:].bitcast(FP8X4), scales=scales[:], in_=w1_grouped[e][:])
+            w1_q[e] = (codes, scales)
+
+        def stage_c(e):
+            codes, scales = w1_q[e]
+            acc = psum1.tile([P, 4, C], F32, tag="ps1")
+            for t in range(4):
+                nc.tensor.matmul_mx(
+                    out=acc[:, t, :],
+                    lhsT=codes[:, t * P:(t + 1) * P].bitcast(FP8X4),
+                    lhsT_scale=scales[:, t * P:(t + 1) * P],
+                    rhs=slot_codes[:, e * C:(e + 1) * C].bitcast(FP8X4),
+                    rhs_scale=slot_scales[:, e * C:(e + 1) * C],
+                    start=True,
+                    stop=True,
+                )
+            l1_acc[e] = acc
+
+        def stage_d(e):
+            h_grouped = quant.tile([P, PACK * C], BF16, tag="hg", align_bytes=64)
+            nc.scalar.activation(
+                out=h_grouped[:].rearrange("p (c t) -> p c t", t=4),
+                in_=l1_acc[e][:].rearrange("p t c -> p c t"),
+                func=SILU,
+            )
+            l1_acc[e] = h_grouped
+
+        def stage_f(e):
+            h_codes = quant.tile([P, C], U32, tag="hc", align_bytes=64)
+            h_scales = quant.tile([P, C], U8, tag="hs", align_bytes=64)
+            nc.vector.quantize_mx(out=h_codes[:].bitcast(FP8X4), scales=h_scales[:], in_=l1_acc[e][:])
+            h_q[e] = (h_codes, h_scales)
+
+        def stage_g(e):
+            grouped = stage.tile([P, PACK * N], BF16, tag="grouped", align_bytes=64)
+            raw = raw_of[(2, e)]
+            if e < E - 2:
+                plain_interleave(nc.scalar.copy, grouped, raw, 0, N)
+            elif e == E - 2:
+                plain_interleave(nc.vector.tensor_copy, grouped, raw, 0, N // 2)
+                plain_interleave(nc.scalar.copy, grouped, raw, N // 2, N)
+            else:
+                plain_interleave(nc.vector.tensor_copy, grouped, raw, 0, P)
+                for nb in range(1, NB):
+                    plain_interleave(nc.scalar.copy, grouped, raw, nb * P, (nb + 1) * P)
+            w2_grouped[e] = grouped
+
+        def stage_hq(e):
+            codes = quant.tile([P, N], U32, tag="w2c", align_bytes=64)
+            scales = quant.tile([P, N], U8, tag="w2s", align_bytes=64)
+            grouped = w2_grouped[e]
+            step = P if e == E - 1 else N
+            for c0 in range(0, N, step):
+                c1 = c0 + step
+                nc.vector.quantize_mx(
+                    out=codes[:, c0:c1].bitcast(FP8X4), scales=scales[:, c0:c1], in_=grouped[:, PACK * c0:PACK * c1]
+                )
+            w2_q[e] = (codes, scales)
+
+        def stage_l(e):
+            codes, scales = w2_q[e]
+            h_codes, h_scales = h_q[e]
+            q = e % GROUP
+            for nb in range(NB):
+                if q == 0:
+                    y_acc[nb] = psum2.tile([P, GROUP * C], F32, tag="yb%d" % nb, name="yb%d" % nb)
+                nc.tensor.matmul_mx(
+                    out=y_acc[nb][:, q * C:(q + 1) * C],
+                    lhsT=codes[:, nb * P:(nb + 1) * P].bitcast(FP8X4),
+                    lhsT_scale=scales[:, nb * P:(nb + 1) * P],
+                    rhs=h_codes[:].bitcast(FP8X4),
+                    rhs_scale=h_scales[:],
+                    start=True,
+                    stop=True,
+                )
+
+        def stage_y(e, nb, copy, experts):
+            s0 = (e + 1 - experts) * C
+            q0 = s0 % (GROUP * C)
+            copy(out=y_sb[nb][:, s0:s0 + experts * C], in_=y_acc[nb][:, q0:q0 + experts * C])
+
+        plain_interleave(nc.vector.tensor_copy, x_grouped, x_raw, 0, T // 2)
+        plain_interleave(nc.scalar.copy, x_grouped, x_raw, T // 2, T)
+        stage_a(0, nc.scalar.copy)
+        nc.vector.quantize_mx(out=x_codes[:].bitcast(FP8X4), scales=x_scales[:], in_=x_grouped[:])
+        gather(0)
+        stage_a(1, nc.vector.tensor_copy)
+        stage_b(0)
+        stage_c(0)
+        stage_d(0)
+        gather(1)
+        gather(2)
+
+        for e in range(E):
+            stage_g(e)
+            if e + 2 < E:
+                stage_a(e + 2, nc.vector.tensor_copy)
+            stage_f(e)
+            if e + 1 < E:
+                stage_b(e + 1)
+                stage_c(e + 1)
+                stage_d(e + 1)
+            stage_hq(e)
+            stage_l(e)
+            if e == GROUP - 1:
+                for nb in range(NB):
+                    stage_y(e, nb, nc.vector.tensor_copy, GROUP)
+            if e == E - 3:
+                for nb in range(NB):
+                    stage_y(e, nb, nc.scalar.copy, 2)
+
+        for nb in range(NB):
+            stage_y(E - 1, nb, nc.vector.tensor_copy if nb == 0 else nc.scalar.copy, 2)
+
+        for nb in range(NB):
+            first = comb.tile([P, T], F32, tag="first")
+            nc.vector.tensor_tensor(first[:], y_sb[nb][:].indirect(pos1_t[:]), gate_t[nb][:, 0, :], MULT)
+            second = comb.tile([P, T], F32, tag="second")
+            nc.vector.tensor_tensor(second[:], y_sb[nb][:].indirect(pos2_t[:]), gate_t[nb][:, 1, :], MULT)
+            total = comb.tile([P, T], F32, tag="total")
+            if nb < NB - 1:
+                acc = psum3.tile([P, T], F32, tag="sum")
+                nc.tensor.matmul(acc[:], ident[:], first[:], start=True, stop=False)
+                nc.tensor.matmul(acc[:], ident[:], second[:], start=False, stop=True)
+                nc.scalar.copy(out=total[:], in_=acc[:])
+            else:
+                nc.vector.tensor_tensor(total[:], first[:], second[:], ADD)
+            nc.sync.dma_start(out=out[nb * P:(nb + 1) * P, :], in_=total[:])

@@ -232,13 +232,19 @@ def tile_routed_moe_kernel(tc, xT, w1, w2, gate, offs, pos1, pos2, out):
             first = comb.tile([P, T], F32, tag="first")
             nc.vector.tensor_tensor(first[:], y_sb[nb][:].indirect(pos1_t[:]), gate_t[nb][:, 0, :], MULT)
             second = comb.tile([P, T], F32, tag="second")
-            nc.vector.tensor_tensor(second[:], y_sb[nb][:].indirect(pos2_t[:]), gate_t[nb][:, 1, :], MULT)
             total = comb.tile([P, T], F32, tag="total")
             if nb < NB - 1:
+                nc.vector.tensor_tensor(second[:], y_sb[nb][:].indirect(pos2_t[:]), gate_t[nb][:, 1, :], MULT)
                 acc = psum3.tile([P, T], F32, tag="sum")
                 nc.tensor.matmul(acc[:], ident[:], first[:], start=True, stop=False)
                 nc.tensor.matmul(acc[:], ident[:], second[:], start=False, stop=True)
                 nc.scalar.copy(out=total[:], in_=acc[:])
+                nc.sync.dma_start(out=out[nb * P:(nb + 1) * P, :], in_=total[:])
             else:
-                nc.vector.tensor_tensor(total[:], first[:], second[:], ADD)
-            nc.sync.dma_start(out=out[nb * P:(nb + 1) * P, :], in_=total[:])
+                for t0 in range(0, T, T // 2):
+                    t1 = t0 + T // 2
+                    nc.vector.tensor_tensor(
+                        second[:, t0:t1], y_sb[nb][:].indirect(pos2_t[:, t0 // 16:t1 // 16]), gate_t[nb][:, 1, t0:t1], MULT
+                    )
+                    nc.vector.tensor_tensor(total[:, t0:t1], first[:, t0:t1], second[:, t0:t1], ADD)
+                    nc.sync.dma_start(out=out[nb * P:(nb + 1) * P, t0:t1], in_=total[:, t0:t1])

@@ -220,7 +220,7 @@ def tile_routed_moe_kernel(tc, xT, w1, w2, gate, offs, pos1, pos2, out):
             stage_l(e)
             if e == GROUP - 1:
                 for nb in range(NB):
-                    stage_y(e, nb, nc.vector.tensor_copy, GROUP)
+                    stage_y(e, nb, nc.scalar.copy, GROUP)
             if e == E - 3:
                 for nb in range(NB):
                     stage_y(e, nb, nc.scalar.copy, 2)

@@ -54,8 +54,13 @@ def tile_routed_moe_kernel(tc, xT, w1, w2, gate, offs, pos1, pos2, out):
                 order.append((1, e + 1))
             order.append((2, e))
         raw_of = {}
-        for which, e in order:
+        for which, e in order[:-1]:
             raw_of[(which, e)] = load_matrix(w1 if which == 1 else w2, e)
+        last_halves = []
+        for c0 in (0, N // 2):
+            half = raws.tile([P, PACK, N // 2], F32, tag="raw", name="half%d" % c0)
+            nc.sync.dma_start(out=half[:], in_=w2[E - 1].rearrange("(p j) c -> p j c", j=PACK)[:, :, c0:c0 + N // 2])
+            last_halves.append(half)
 
         pos1_t = lists.tile([P, T // 16], U16, name="pos1_t")
         nc.sync.dma_start(pos1_t[:], pos1)
@@ -152,32 +157,22 @@ def tile_routed_moe_kernel(tc, xT, w1, w2, gate, offs, pos1, pos2, out):
             raw = raw_of[(2, e)]
             if e < E - 2:
                 plain_interleave(nc.scalar.copy, grouped, raw, 0, N)
-            elif e == E - 2:
-                plain_interleave(nc.vector.tensor_copy, grouped, raw, 0, N // 2)
-                plain_interleave(nc.scalar.copy, grouped, raw, N // 2, N)
             else:
                 plain_interleave(nc.vector.tensor_copy, grouped, raw, 0, P)
-                for nb in range(1, NB):
-                    plain_interleave(nc.scalar.copy, grouped, raw, nb * P, (nb + 1) * P)
+                plain_interleave(nc.scalar.copy, grouped, raw, P, N)
             w2_grouped[e] = grouped
 
         def stage_hq(e):
             codes = quant.tile([P, N], U32, tag="w2c", align_bytes=64)
             scales = quant.tile([P, N], U8, tag="w2s", align_bytes=64)
-            grouped = w2_grouped[e]
-            step = P if e == E - 1 else N
-            for c0 in range(0, N, step):
-                c1 = c0 + step
-                nc.vector.quantize_mx(
-                    out=codes[:, c0:c1].bitcast(FP8X4), scales=scales[:, c0:c1], in_=grouped[:, PACK * c0:PACK * c1]
-                )
+            nc.vector.quantize_mx(out=codes[:].bitcast(FP8X4), scales=scales[:], in_=w2_grouped[e][:])
             w2_q[e] = (codes, scales)
 
-        def stage_l(e):
+        def stage_l(e, blocks):
             codes, scales = w2_q[e]
             h_codes, h_scales = h_q[e]
             q = e % GROUP
-            for nb in range(NB):
+            for nb in blocks:
                 if q == 0:
                     y_acc[nb] = psum2.tile([P, GROUP * C], F32, tag="yb%d" % nb, name="yb%d" % nb)
                 nc.tensor.matmul_mx(
@@ -189,6 +184,28 @@ def tile_routed_moe_kernel(tc, xT, w1, w2, gate, offs, pos1, pos2, out):
                     start=True,
                     stop=True,
                 )
+
+        def last_half(i, copy):
+            e = E - 1
+            if i == 0:
+                w2_grouped[e] = stage.tile([P, PACK * N], BF16, tag="grouped", name="grouped_last", align_bytes=64)
+                codes = quant.tile([P, N], U32, tag="w2c", align_bytes=64)
+                scales = quant.tile([P, N], U8, tag="w2s", align_bytes=64)
+                w2_q[e] = (codes, scales)
+            c0 = i * N // 2
+            c1 = c0 + N // 2
+            codes, scales = w2_q[e]
+            grouped = w2_grouped[e]
+            copy(
+                out=grouped[:, PACK * c0:PACK * c1].rearrange("p (c i j) -> p c j i", i=4, j=PACK),
+                in_=last_halves[i][:].rearrange("p j (c i) -> p c j i", i=4),
+            )
+            if i == 0:
+                stage_f(e)
+            nc.vector.quantize_mx(
+                out=codes[:, c0:c1].bitcast(FP8X4), scales=scales[:, c0:c1], in_=grouped[:, PACK * c0:PACK * c1]
+            )
+            stage_l(e, (2 * i, 2 * i + 1))
 
         def stage_y(e, nb, copy, experts):
             s0 = (e + 1 - experts) * C
@@ -207,26 +224,25 @@ def tile_routed_moe_kernel(tc, xT, w1, w2, gate, offs, pos1, pos2, out):
         gather(1)
         gather(2)
 
-        for e in range(E):
+        for e in range(E - 1):
             stage_g(e)
             if e + 2 < E:
                 stage_a(e + 2, nc.vector.tensor_copy)
             stage_f(e)
-            if e + 1 < E:
-                stage_b(e + 1)
-                stage_c(e + 1)
-                stage_d(e + 1)
+            stage_b(e + 1)
+            stage_c(e + 1)
+            stage_d(e + 1)
             stage_hq(e)
-            stage_l(e)
+            stage_l(e, range(NB))
             if e == GROUP - 1:
                 for nb in range(NB):
-                    stage_y(e, nb, nc.scalar.copy, GROUP)
-            if e == E - 3:
-                for nb in range(NB):
-                    stage_y(e, nb, nc.scalar.copy, 2)
-
-        for nb in range(NB):
-            stage_y(E - 1, nb, nc.vector.tensor_copy if nb == 0 else nc.scalar.copy, 2)
+                    stage_y(e, nb, nc.vector.tensor_copy, GROUP)
+        last_half(0, nc.vector.tensor_copy)
+        for nb in (0, 1):
+            stage_y(E - 1, nb, nc.scalar.copy, GROUP)
+        last_half(1, nc.scalar.copy)
+        for nb in (2, 3):
+            stage_y(E - 1, nb, nc.scalar.copy, GROUP)
 
         for nb in range(NB):
             first = comb.tile([P, T], F32, tag="first")

@@ -236,31 +236,33 @@ def tile_routed_moe_kernel(tc, xT, w1, w2, gate, offs, pos1, pos2, out):
             stage_l(e, range(NB))
             if e == GROUP - 1:
                 for nb in range(NB):
-                    stage_y(e, nb, nc.vector.tensor_copy, GROUP)
+                    stage_y(e, nb, nc.scalar.copy, GROUP)
+            if e == E - 3:
+                stage_y(e, 0, nc.scalar.copy, 2)
         last_half(0, nc.vector.tensor_copy)
-        for nb in (0, 1):
-            stage_y(E - 1, nb, nc.scalar.copy, GROUP)
-        last_half(1, nc.scalar.copy)
+        stage_y(E - 1, 0, nc.scalar.copy, 2)
+        stage_y(E - 1, 1, nc.scalar.copy, GROUP)
+        last_half(1, nc.vector.tensor_copy)
         for nb in (2, 3):
             stage_y(E - 1, nb, nc.scalar.copy, GROUP)
 
+        half = T // 2
         for nb in range(NB):
             first = comb.tile([P, T], F32, tag="first")
             nc.vector.tensor_tensor(first[:], y_sb[nb][:].indirect(pos1_t[:]), gate_t[nb][:, 0, :], MULT)
             second = comb.tile([P, T], F32, tag="second")
             total = comb.tile([P, T], F32, tag="total")
-            if nb < NB - 1:
-                nc.vector.tensor_tensor(second[:], y_sb[nb][:].indirect(pos2_t[:]), gate_t[nb][:, 1, :], MULT)
-                acc = psum3.tile([P, T], F32, tag="sum")
-                nc.tensor.matmul(acc[:], ident[:], first[:], start=True, stop=False)
-                nc.tensor.matmul(acc[:], ident[:], second[:], start=False, stop=True)
-                nc.scalar.copy(out=total[:], in_=acc[:])
-                nc.sync.dma_start(out=out[nb * P:(nb + 1) * P, :], in_=total[:])
-            else:
-                for t0 in range(0, T, T // 2):
-                    t1 = t0 + T // 2
-                    nc.vector.tensor_tensor(
-                        second[:, t0:t1], y_sb[nb][:].indirect(pos2_t[:, t0 // 16:t1 // 16]), gate_t[nb][:, 1, t0:t1], MULT
-                    )
+            for engine, t0, t1 in ((("T", 0, T),), (("T", 0, T),), (("T", 0, 3 * T // 4), ("V", 3 * T // 4, T)), (("V", 0, half), ("V", half, T)))[nb]:
+                nc.vector.tensor_tensor(
+                    second[:, t0:t1], y_sb[nb][:].indirect(pos2_t[:, t0 // 16:t1 // 16]), gate_t[nb][:, 1, t0:t1], MULT
+                )
+                rows = out[nb * P:(nb + 1) * P, t0:t1]
+                if engine == "T":
+                    acc = psum3.tile([P, T], F32, tag="sum")
+                    nc.tensor.matmul(acc[:, t0:t1], ident[:], first[:, t0:t1], start=True, stop=False)
+                    nc.tensor.matmul(acc[:, t0:t1], ident[:], second[:, t0:t1], start=False, stop=True)
+                    nc.scalar.copy(out=total[:, t0:t1], in_=acc[:, t0:t1])
+                    nc.scalar.dma_start(out=rows, in_=total[:, t0:t1])
+                else:
                     nc.vector.tensor_tensor(total[:, t0:t1], first[:, t0:t1], second[:, t0:t1], ADD)
-                    nc.sync.dma_start(out=out[nb * P:(nb + 1) * P, t0:t1], in_=total[:, t0:t1])
+                    nc.sync.dma_start(out=rows, in_=total[:, t0:t1])

@@ -252,7 +252,7 @@ def tile_routed_moe_kernel(tc, xT, w1, w2, gate, offs, pos1, pos2, out):
             nc.vector.tensor_tensor(first[:], y_sb[nb][:].indirect(pos1_t[:]), gate_t[nb][:, 0, :], MULT)
             second = comb.tile([P, T], F32, tag="second")
             total = comb.tile([P, T], F32, tag="total")
-            for engine, t0, t1 in ((("T", 0, T),), (("T", 0, T),), (("T", 0, 3 * T // 4), ("V", 3 * T // 4, T)), (("V", 0, half), ("V", half, T)))[nb]:
+            for engine, t0, t1 in ((("T", 0, T),), (("T", 0, T),), (("T", 0, half), ("V", half, T)), (("V", 0, half), ("V", half, T)))[nb]:
                 nc.vector.tensor_tensor(
                     second[:, t0:t1], y_sb[nb][:].indirect(pos2_t[:, t0 // 16:t1 // 16]), gate_t[nb][:, 1, t0:t1], MULT
                 )

@@ -19,9 +19,11 @@ ADD = mybir.AluOpType.add
 P = 128
 PACK = 4
 NB = N // P
-RAW_BUFS = 14
+RAW_BUFS = 11
 GATHER_CUTS = (0, 256, 640, 1024)
 GROUP = 4
+LATE = {(1, E - 2): "w1_6", (1, E - 1): "w1_7", (2, E - 2): "w2_6"}
+H_TAKES = {E - 3: "g2_4", E - 2: "w1_7", E - 1: "w2_6"}
 
 
 def tile_routed_moe_kernel(tc, xT, w1, w2, gate, offs, pos1, pos2, out):
@@ -33,6 +35,7 @@ def tile_routed_moe_kernel(tc, xT, w1, w2, gate, offs, pos1, pos2, out):
         stage = ctx.enter_context(tc.tile_pool(name="stage", bufs=5))
         quant = ctx.enter_context(tc.tile_pool(name="quant", bufs=3))
         comb = ctx.enter_context(tc.tile_pool(name="comb", bufs=3))
+        shared = ctx.enter_context(tc.tile_pool(name="shared", bufs=1))
         psum1 = ctx.enter_context(tc.psum_pool(name="psum1", bufs=2))
         psum2 = ctx.enter_context(tc.psum_pool(name="psum2", bufs=1))
         psum3 = ctx.enter_context(tc.psum_pool(name="psum3", bufs=2))
@@ -44,7 +47,11 @@ def tile_routed_moe_kernel(tc, xT, w1, w2, gate, offs, pos1, pos2, out):
         nc.sync.dma_start(out=x_raw[:], in_=xT.rearrange("(p j) t -> p j t", j=PACK))
 
         def load_matrix(w, e):
-            raw = raws.tile([P, PACK, 512], F32, tag="raw")
+            late = LATE.get((1 if w is w1 else 2, e))
+            if late:
+                raw = shared.tile([P, PACK, 512], F32, tag=late, name="raw_late", align_bytes=64)
+            else:
+                raw = raws.tile([P, PACK, 512], F32, tag="raw", name="raw")
             nc.sync.dma_start(out=raw[:], in_=w[e].rearrange("(p j) c -> p j c", j=PACK))
             return raw
 
@@ -147,23 +154,32 @@ def tile_routed_moe_kernel(tc, xT, w1, w2, gate, offs, pos1, pos2, out):
             l1_acc[e] = h_grouped
 
         def stage_f(e):
-            h_codes = quant.tile([P, C], U32, tag="hc", align_bytes=64)
+            if e in H_TAKES:
+                h_codes = shared.tile([P, C], U32, tag=H_TAKES[e], name="h_codes_late", align_bytes=64)
+            else:
+                h_codes = quant.tile([P, C], U32, tag="hc", name="h_codes", align_bytes=64)
             h_scales = quant.tile([P, C], U8, tag="hs", align_bytes=64)
             nc.vector.quantize_mx(out=h_codes[:].bitcast(FP8X4), scales=h_scales[:], in_=l1_acc[e][:])
             h_q[e] = (h_codes, h_scales)
 
         def stage_g(e):
-            grouped = stage.tile([P, PACK * N], BF16, tag="grouped", align_bytes=64)
-            raw = raw_of[(2, e)]
-            if e < E - 2:
-                plain_interleave(nc.scalar.copy, grouped, raw, 0, N)
+            if e == E - 4:
+                grouped = shared.tile([P, PACK * N], BF16, tag="g2_4", name="grouped_late", align_bytes=64)
             else:
-                plain_interleave(nc.vector.tensor_copy, grouped, raw, 0, P)
-                plain_interleave(nc.scalar.copy, grouped, raw, P, N)
+                grouped = stage.tile([P, PACK * N], BF16, tag="grouped", name="grouped", align_bytes=64)
+            raw = raw_of[(2, e)]
+            split = {E - 4: P, E - 3: 2 * P, E - 2: N}.get(e, 0)
+            if split > 0:
+                plain_interleave(nc.vector.tensor_copy, grouped, raw, 0, split)
+            if split < N:
+                plain_interleave(nc.scalar.copy, grouped, raw, split, N)
             w2_grouped[e] = grouped
 
         def stage_hq(e):
-            codes = quant.tile([P, N], U32, tag="w2c", align_bytes=64)
+            if e == E - 4:
+                codes = shared.tile([P, N], U32, tag="w1_6", name="codes_late", align_bytes=64)
+            else:
+                codes = quant.tile([P, N], U32, tag="w2c", name="codes", align_bytes=64)
             scales = quant.tile([P, N], U8, tag="w2s", align_bytes=64)
             nc.vector.quantize_mx(out=codes[:].bitcast(FP8X4), scales=scales[:], in_=w2_grouped[e][:])
             w2_q[e] = (codes, scales)
@@ -185,7 +201,7 @@ def tile_routed_moe_kernel(tc, xT, w1, w2, gate, offs, pos1, pos2, out):
                     stop=True,
                 )
 
-        def last_half(i, copy):
+        def last_half(i, shares):
             e = E - 1
             if i == 0:
                 w2_grouped[e] = stage.tile([P, PACK * N], BF16, tag="grouped", name="grouped_last", align_bytes=64)
@@ -196,10 +212,11 @@ def tile_routed_moe_kernel(tc, xT, w1, w2, gate, offs, pos1, pos2, out):
             c1 = c0 + N // 2
             codes, scales = w2_q[e]
             grouped = w2_grouped[e]
-            copy(
-                out=grouped[:, PACK * c0:PACK * c1].rearrange("p (c i j) -> p c j i", i=4, j=PACK),
-                in_=last_halves[i][:].rearrange("p j (c i) -> p c j i", i=4),
-            )
+            for copy, a, b in shares:
+                copy(
+                    out=grouped[:, PACK * (c0 + a):PACK * (c0 + b)].rearrange("p (c i j) -> p c j i", i=4, j=PACK),
+                    in_=last_halves[i][:, :, a:b].rearrange("p j (c i) -> p c j i", i=4),
+                )
             if i == 0:
                 stage_f(e)
             nc.vector.quantize_mx(
@@ -239,10 +256,10 @@ def tile_routed_moe_kernel(tc, xT, w1, w2, gate, offs, pos1, pos2, out):
                     stage_y(e, nb, nc.scalar.copy, GROUP)
             if e == E - 3:
                 stage_y(e, 0, nc.scalar.copy, 2)
-        last_half(0, nc.vector.tensor_copy)
+        last_half(0, ((nc.scalar.copy, 0, P), (nc.vector.tensor_copy, P, 2 * P)))
         stage_y(E - 1, 0, nc.scalar.copy, 2)
         stage_y(E - 1, 1, nc.scalar.copy, GROUP)
-        last_half(1, nc.vector.tensor_copy)
+        last_half(1, ((nc.vector.tensor_copy, 0, 2 * P),))
         for nb in (2, 3):
             stage_y(E - 1, nb, nc.scalar.copy, GROUP)
 

@@ -22,6 +22,7 @@ NB = N // P
 RAW_BUFS = 11
 GATHER_CUTS = (0, 256, 640, 1024)
 GROUP = 4
+HALVED = {(1, E - 1), (2, E - 2)}
 LATE = {(1, E - 2): "w1_6", (1, E - 1): "w1_7", (2, E - 2): "w2_6"}
 H_TAKES = {E - 3: "g2_4", E - 2: "w1_7", E - 1: "w2_6"}
 
@@ -69,16 +70,15 @@ def tile_routed_moe_kernel(tc, xT, w1, w2, gate, offs, pos1, pos2, out):
             nc.sync.dma_start(out=half[:], in_=w2[E - 1].rearrange("(p j) c -> p j c", j=PACK)[:, :, c0:c0 + N // 2])
             last_halves.append(half)
 
+        gate_t = [raws.tile([P, 2, T], F32, tag="raw", name="gate_t%d" % nb) for nb in range(NB)]
         pos1_t = lists.tile([P, T // 16], U16, name="pos1_t")
         nc.sync.dma_start(pos1_t[:], pos1)
+        nc.sync.dma_start(out=gate_t[0][:, 0, :], in_=gate[0, 0:P, :])
         pos2_t = lists.tile([P, T // 16], U16, name="pos2_t")
         nc.sync.dma_start(pos2_t[:], pos2)
-
-        gate_t = []
-        for nb in range(NB):
-            g = raws.tile([P, 2, T], F32, tag="raw", name="gate_t%d" % nb)
-            nc.sync.dma_start(out=g[:], in_=gate[:, nb * P:(nb + 1) * P, :].rearrange("r p t -> p r t"))
-            gate_t.append(g)
+        nc.sync.dma_start(out=gate_t[0][:, 1, :], in_=gate[1, 0:P, :])
+        for nb in range(1, NB):
+            nc.sync.dma_start(out=gate_t[nb][:], in_=gate[:, nb * P:(nb + 1) * P, :].rearrange("r p t -> p r t"))
 
         ident = keep.tile([P, P], F32, name="ident")
         make_identity(nc, ident[:])
@@ -115,18 +115,30 @@ def tile_routed_moe_kernel(tc, xT, w1, w2, gate, offs, pos1, pos2, out):
         w2_q = {}
         y_acc = {}
 
+        def pieces(which, e):
+            n = 2 if (which, e) in HALVED else 1
+            tag = "grouped" if n == 1 else "grouped_half"
+            return [stage.tile([P, PACK * 512 // n], BF16, tag=tag, name=tag, align_bytes=64) for i in range(n)]
+
+        def quantise(codes, scales, grouped):
+            w = grouped[0].shape[1] // PACK
+            for i, piece in enumerate(grouped):
+                cols = slice(i * w, (i + 1) * w)
+                nc.vector.quantize_mx(out=codes[:, cols].bitcast(FP8X4), scales=scales[:, cols], in_=piece[:])
+
         def stage_a(e, copy):
-            grouped = stage.tile([P, PACK * H], BF16, tag="grouped", align_bytes=64)
-            copy(
-                out=grouped[:].rearrange("p (t m j) -> p m j t", t=4, j=PACK),
-                in_=raw_of[(1, e)][:].rearrange("p j (m t) -> p m j t", t=4),
-            )
-            w1_grouped[e] = grouped
+            w1_grouped[e] = pieces(1, e)
+            nt = 4 // len(w1_grouped[e])
+            for i, piece in enumerate(w1_grouped[e]):
+                copy(
+                    out=piece[:].rearrange("p (t m j) -> p m j t", t=nt, j=PACK),
+                    in_=raw_of[(1, e)][:].rearrange("p j (m t) -> p m j t", t=4)[:, :, :, i * nt:(i + 1) * nt],
+                )
 
         def stage_b(e):
             codes = quant.tile([P, H], U32, tag="w1c", align_bytes=64)
             scales = quant.tile([P, H], U8, tag="w1s", align_bytes=64)
-            nc.vector.quantize_mx(out=codes[:].bitcast(FP8X4), scales=scales[:], in_=w1_grouped[e][:])
+            quantise(codes, scales, w1_grouped[e])
             w1_q[e] = (codes, scales)
 
         def stage_c(e):
@@ -143,6 +155,18 @@ def tile_routed_moe_kernel(tc, xT, w1, w2, gate, offs, pos1, pos2, out):
                     stop=True,
                 )
             l1_acc[e] = acc
+
+        def keep_busy(codes, scales):
+            idle = psum3.tile([P, T], F32, tag="sum", name="idle")
+            nc.tensor.matmul_mx(
+                out=idle[:],
+                lhsT=codes[:, 0:P].bitcast(FP8X4),
+                lhsT_scale=scales[:, 0:P],
+                rhs=slot_codes[:, 0:T].bitcast(FP8X4),
+                rhs_scale=slot_scales[:, 0:T],
+                start=True,
+                stop=True,
+            )
 
         def stage_d(e):
             h_grouped = quant.tile([P, PACK * C], BF16, tag="hg", align_bytes=64)
@@ -163,17 +187,23 @@ def tile_routed_moe_kernel(tc, xT, w1, w2, gate, offs, pos1, pos2, out):
             h_q[e] = (h_codes, h_scales)
 
         def stage_g(e):
+            raw = raw_of[(2, e)]
+            if (2, e) in HALVED:
+                w2_grouped[e] = pieces(2, e)
+                w = N // len(w2_grouped[e])
+                for i, piece in enumerate(w2_grouped[e]):
+                    plain_interleave(nc.vector.tensor_copy, piece, raw[:, :, i * w:(i + 1) * w], 0, w)
+                return
             if e == E - 4:
                 grouped = shared.tile([P, PACK * N], BF16, tag="g2_4", name="grouped_late", align_bytes=64)
             else:
                 grouped = stage.tile([P, PACK * N], BF16, tag="grouped", name="grouped", align_bytes=64)
-            raw = raw_of[(2, e)]
-            split = {E - 4: P, E - 3: 2 * P, E - 2: N}.get(e, 0)
+            split = {E - 4: P, E - 3: 2 * P}.get(e, 0)
             if split > 0:
                 plain_interleave(nc.vector.tensor_copy, grouped, raw, 0, split)
             if split < N:
                 plain_interleave(nc.scalar.copy, grouped, raw, split, N)
-            w2_grouped[e] = grouped
+            w2_grouped[e] = [grouped]
 
         def stage_hq(e):
             if e == E - 4:
@@ -181,10 +211,10 @@ def tile_routed_moe_kernel(tc, xT, w1, w2, gate, offs, pos1, pos2, out):
             else:
                 codes = quant.tile([P, N], U32, tag="w2c", name="codes", align_bytes=64)
             scales = quant.tile([P, N], U8, tag="w2s", align_bytes=64)
-            nc.vector.quantize_mx(out=codes[:].bitcast(FP8X4), scales=scales[:], in_=w2_grouped[e][:])
+            quantise(codes, scales, w2_grouped[e])
             w2_q[e] = (codes, scales)
 
-        def stage_l(e, blocks):
+        def stage_l(e, blocks, first=0):
             codes, scales = w2_q[e]
             h_codes, h_scales = h_q[e]
             q = e % GROUP
@@ -193,8 +223,8 @@ def tile_routed_moe_kernel(tc, xT, w1, w2, gate, offs, pos1, pos2, out):
                     y_acc[nb] = psum2.tile([P, GROUP * C], F32, tag="yb%d" % nb, name="yb%d" % nb)
                 nc.tensor.matmul_mx(
                     out=y_acc[nb][:, q * C:(q + 1) * C],
-                    lhsT=codes[:, nb * P:(nb + 1) * P].bitcast(FP8X4),
-                    lhsT_scale=scales[:, nb * P:(nb + 1) * P],
+                    lhsT=codes[:, (nb - first) * P:(nb - first + 1) * P].bitcast(FP8X4),
+                    lhsT_scale=scales[:, (nb - first) * P:(nb - first + 1) * P],
                     rhs=h_codes[:].bitcast(FP8X4),
                     rhs_scale=h_scales[:],
                     start=True,
@@ -203,26 +233,19 @@ def tile_routed_moe_kernel(tc, xT, w1, w2, gate, offs, pos1, pos2, out):
 
         def last_half(i, shares):
             e = E - 1
-            if i == 0:
-                w2_grouped[e] = stage.tile([P, PACK * N], BF16, tag="grouped", name="grouped_last", align_bytes=64)
-                codes = quant.tile([P, N], U32, tag="w2c", align_bytes=64)
-                scales = quant.tile([P, N], U8, tag="w2s", align_bytes=64)
-                w2_q[e] = (codes, scales)
-            c0 = i * N // 2
-            c1 = c0 + N // 2
-            codes, scales = w2_q[e]
-            grouped = w2_grouped[e]
+            pieces_of = []
             for copy, a, b in shares:
-                copy(
-                    out=grouped[:, PACK * (c0 + a):PACK * (c0 + b)].rearrange("p (c i j) -> p c j i", i=4, j=PACK),
-                    in_=last_halves[i][:, :, a:b].rearrange("p j (c i) -> p c j i", i=4),
-                )
+                piece = stage.tile([P, PACK * (b - a)], BF16, tag="last%d" % (b - a), name="last%d" % (b - a), align_bytes=64)
+                plain_interleave(copy, piece, last_halves[i][:, :, a:b], 0, b - a)
+                pieces_of.append((piece, a, b))
             if i == 0:
                 stage_f(e)
-            nc.vector.quantize_mx(
-                out=codes[:, c0:c1].bitcast(FP8X4), scales=scales[:, c0:c1], in_=grouped[:, PACK * c0:PACK * c1]
-            )
-            stage_l(e, (2 * i, 2 * i + 1))
+            for piece, a, b in pieces_of:
+                codes = quant.tile([P, b - a], U32, tag="last_c%d" % i, name="last_c", align_bytes=64)
+                scales = quant.tile([P, b - a], U8, tag="last_s%d" % i, name="last_s", align_bytes=64)
+                quantise(codes, scales, [piece])
+                w2_q[e] = (codes, scales)
+                stage_l(e, range((2 * i * P + a) // P, (2 * i * P + b) // P), (2 * i * P + a) // P)
 
         def stage_y(e, nb, copy, experts):
             s0 = (e + 1 - experts) * C
@@ -248,6 +271,8 @@ def tile_routed_moe_kernel(tc, xT, w1, w2, gate, offs, pos1, pos2, out):
             stage_f(e)
             stage_b(e + 1)
             stage_c(e + 1)
+            if e + 1 == E - 1:
+                keep_busy(*w1_q[e + 1])
             stage_d(e + 1)
             stage_hq(e)
             stage_l(e, range(NB))
@@ -259,7 +284,9 @@ def tile_routed_moe_kernel(tc, xT, w1, w2, gate, offs, pos1, pos2, out):
         last_half(0, ((nc.scalar.copy, 0, P), (nc.vector.tensor_copy, P, 2 * P)))
         stage_y(E - 1, 0, nc.scalar.copy, 2)
         stage_y(E - 1, 1, nc.scalar.copy, GROUP)
-        last_half(1, ((nc.vector.tensor_copy, 0, 2 * P),))
+        last_half(1, ((nc.vector.tensor_copy, 0, P), (nc.vector.tensor_copy, P, 2 * P)))
+        for i in range(2):
+            keep_busy(*w2_q[E - 1])
         for nb in (2, 3):
             stage_y(E - 1, nb, nc.scalar.copy, GROUP)
 
@@ -269,7 +296,7 @@ def tile_routed_moe_kernel(tc, xT, w1, w2, gate, offs, pos1, pos2, out):
             nc.vector.tensor_tensor(first[:], y_sb[nb][:].indirect(pos1_t[:]), gate_t[nb][:, 0, :], MULT)
             second = comb.tile([P, T], F32, tag="second")
             total = comb.tile([P, T], F32, tag="total")
-            for engine, t0, t1 in ((("T", 0, T),), (("T", 0, T),), (("T", 0, half), ("V", half, T)), (("V", 0, half), ("V", half, T)))[nb]:
+            for engine, t0, t1 in ((("T", 0, T),), (("T", 0, T),), (("T", 0, half), ("T", half, T)), (("V", 0, half), ("V", half, T)))[nb]:
                 nc.vector.tensor_tensor(
                     second[:, t0:t1], y_sb[nb][:].indirect(pos2_t[:, t0 // 16:t1 // 16]), gate_t[nb][:, 1, t0:t1], MULT
                 )

@@ -156,18 +156,6 @@ def tile_routed_moe_kernel(tc, xT, w1, w2, gate, offs, pos1, pos2, out):
                 )
             l1_acc[e] = acc
 
-        def keep_busy(codes, scales):
-            idle = psum3.tile([P, T], F32, tag="sum", name="idle")
-            nc.tensor.matmul_mx(
-                out=idle[:],
-                lhsT=codes[:, 0:P].bitcast(FP8X4),
-                lhsT_scale=scales[:, 0:P],
-                rhs=slot_codes[:, 0:T].bitcast(FP8X4),
-                rhs_scale=slot_scales[:, 0:T],
-                start=True,
-                stop=True,
-            )
-
         def stage_d(e):
             h_grouped = quant.tile([P, PACK * C], BF16, tag="hg", align_bytes=64)
             nc.scalar.activation(
@@ -271,8 +259,6 @@ def tile_routed_moe_kernel(tc, xT, w1, w2, gate, offs, pos1, pos2, out):
             stage_f(e)
             stage_b(e + 1)
             stage_c(e + 1)
-            if e + 1 == E - 1:
-                keep_busy(*w1_q[e + 1])
             stage_d(e + 1)
             stage_hq(e)
             stage_l(e, range(NB))
@@ -285,8 +271,6 @@ def tile_routed_moe_kernel(tc, xT, w1, w2, gate, offs, pos1, pos2, out):
         stage_y(E - 1, 0, nc.scalar.copy, 2)
         stage_y(E - 1, 1, nc.scalar.copy, GROUP)
         last_half(1, ((nc.vector.tensor_copy, 0, P), (nc.vector.tensor_copy, P, 2 * P)))
-        for i in range(2):
-            keep_busy(*w2_q[E - 1])
         for nb in (2, 3):
             stage_y(E - 1, nb, nc.scalar.copy, GROUP)
 
@@ -296,7 +280,7 @@ def tile_routed_moe_kernel(tc, xT, w1, w2, gate, offs, pos1, pos2, out):
             nc.vector.tensor_tensor(first[:], y_sb[nb][:].indirect(pos1_t[:]), gate_t[nb][:, 0, :], MULT)
             second = comb.tile([P, T], F32, tag="second")
             total = comb.tile([P, T], F32, tag="total")
-            for engine, t0, t1 in ((("T", 0, T),), (("T", 0, T),), (("T", 0, half), ("T", half, T)), (("V", 0, half), ("V", half, T)))[nb]:
+            for engine, t0, t1 in ((("T", 0, T),), (("T", 0, T),), (("T", 0, half), ("V", half, T)), (("V", 0, half), ("V", half, T)))[nb]:
                 nc.vector.tensor_tensor(
                     second[:, t0:t1], y_sb[nb][:].indirect(pos2_t[:, t0 // 16:t1 // 16]), gate_t[nb][:, 1, t0:t1], MULT
                 )

from contextlib import ExitStack

import concourse.mybir as mybir
from concourse.masks import make_identity

K, T, E, C, H, N = 512, 512, 8, 128, 512, 512
FLOPS = 2 * E * C * (K * H + H * N)

F32 = mybir.dt.float32
BF16 = mybir.dt.bfloat16
U32 = mybir.dt.uint32
U16 = mybir.dt.uint16
U8 = mybir.dt.uint8
FP8X4 = mybir.dt.float8_e4m3fn_x4
SILU = mybir.ActivationFunctionType.Silu
MULT = mybir.AluOpType.mult
ADD = mybir.AluOpType.add

P = 128
PACK = 4
NB = N // P
RAW_BUFS = 11
GATHER_CUTS = (0, 256, 640, 1024)
GROUP = 4
HALVED = {(1, E - 1), (2, E - 2)}
LATE = {(1, E - 2): "w1_6", (1, E - 1): "w1_7", (2, E - 2): "w2_6"}
H_TAKES = {E - 3: "g2_4", E - 2: "w1_7", E - 1: "w2_6"}


def tile_routed_moe_kernel(tc, xT, w1, w2, gate, offs, pos1, pos2, out):
    nc = tc.nc
    with ExitStack() as ctx:
        lists = ctx.enter_context(tc.tile_pool(name="lists", bufs=1))
        keep = ctx.enter_context(tc.tile_pool(name="keep", bufs=1))
        raws = ctx.enter_context(tc.tile_pool(name="raws", bufs=RAW_BUFS))
        stage = ctx.enter_context(tc.tile_pool(name="stage", bufs=5))
        quant = ctx.enter_context(tc.tile_pool(name="quant", bufs=3))
        comb = ctx.enter_context(tc.tile_pool(name="comb", bufs=3))
        shared = ctx.enter_context(tc.tile_pool(name="shared", bufs=1))
        psum1 = ctx.enter_context(tc.psum_pool(name="psum1", bufs=2))
        psum2 = ctx.enter_context(tc.psum_pool(name="psum2", bufs=1))
        psum3 = ctx.enter_context(tc.psum_pool(name="psum3", bufs=2))

        offs_t = lists.tile([P, E * C // 16], U16, name="offs_t")
        nc.sync.dma_start(offs_t[:], offs)

        x_raw = raws.tile([P, PACK, T], F32, tag="raw")
        nc.sync.dma_start(out=x_raw[:], in_=xT.rearrange("(p j) t -> p j t", j=PACK))

        def load_matrix(w, e):
            late = LATE.get((1 if w is w1 else 2, e))
            if late:
                raw = shared.tile([P, PACK, 512], F32, tag=late, name="raw_late", align_bytes=64)
            else:
                raw = raws.tile([P, PACK, 512], F32, tag="raw", name="raw")
            nc.sync.dma_start(out=raw[:], in_=w[e].rearrange("(p j) c -> p j c", j=PACK))
            return raw

        order = [(1, 0)]
        for e in range(E):
            if e + 1 < E:
                order.append((1, e + 1))
            order.append((2, e))
        raw_of = {}
        for which, e in order[:-1]:
            raw_of[(which, e)] = load_matrix(w1 if which == 1 else w2, e)
        last_halves = []
        for c0 in (0, N // 2):
            half = raws.tile([P, PACK, N // 2], F32, tag="raw", name="half%d" % c0)
            nc.sync.dma_start(out=half[:], in_=w2[E - 1].rearrange("(p j) c -> p j c", j=PACK)[:, :, c0:c0 + N // 2])
            last_halves.append(half)

        gate_t = [raws.tile([P, 2, T], F32, tag="raw", name="gate_t%d" % nb) for nb in range(NB)]
        pos1_t = lists.tile([P, T // 16], U16, name="pos1_t")
        nc.sync.dma_start(pos1_t[:], pos1)
        nc.sync.dma_start(out=gate_t[0][:, 0, :], in_=gate[0, 0:P, :])
        pos2_t = lists.tile([P, T // 16], U16, name="pos2_t")
        nc.sync.dma_start(pos2_t[:], pos2)
        nc.sync.dma_start(out=gate_t[0][:, 1, :], in_=gate[1, 0:P, :])
        for nb in range(1, NB):
            nc.sync.dma_start(out=gate_t[nb][:], in_=gate[:, nb * P:(nb + 1) * P, :].rearrange("r p t -> p r t"))

        ident = keep.tile([P, P], F32, name="ident")
        make_identity(nc, ident[:])

        warm_in = keep.tile([P, 1], F32, name="warm_in")
        warm_out = keep.tile([P, 1], F32, name="warm_out")
        nc.gpsimd.memset(warm_in[:], 0.0)
        nc.scalar.activation(out=warm_out[:], in_=warm_in[:], func=SILU)

        x_codes = keep.tile([P, T], U32, name="x_codes", align_bytes=64)
        x_scales = keep.tile([P, T], U8, name="x_scales", align_bytes=64)
        nc.gpsimd.memset(x_scales[:], 0)
        x_grouped = keep.tile([P, PACK * T], BF16, name="x_grouped", align_bytes=64)
        slot_codes = keep.tile([P, E * C], U32, name="slot_codes", align_bytes=64)
        slot_scales = keep.tile([P, E * C], U8, name="slot_scales", align_bytes=64)
        y_sb = [keep.tile([P, E * C], F32, name="y_sb%d" % nb) for nb in range(NB)]

        def plain_interleave(copy, grouped, raw, c0, c1):
            copy(
                out=grouped[:, PACK * c0:PACK * c1].rearrange("p (c i j) -> p c j i", i=4, j=PACK),
                in_=raw[:, :, c0:c1].rearrange("p j (c i) -> p c j i", i=4),
            )

        def gather(s):
            a, b = GATHER_CUTS[s], GATHER_CUTS[s + 1]
            nc.vector.tensor_copy(slot_codes[:, a:b], x_codes[:].indirect(offs_t[:, a // 16:b // 16]))
            nc.vector.tensor_copy(slot_scales[:, a:b], x_scales[:].indirect(offs_t[:, a // 16:b // 16]))

        w1_grouped = {}
        w1_q = {}
        l1_acc = {}
        h_q = {}
        w2_grouped = {}
        w2_q = {}
        y_acc = {}

        def pieces(which, e):
            n = 2 if (which, e) in HALVED else 1
            tag = "grouped" if n == 1 else "grouped_half"
            return [stage.tile([P, PACK * 512 // n], BF16, tag=tag, name=tag, align_bytes=64) for i in range(n)]

        def quantise(codes, scales, grouped):
            w = grouped[0].shape[1] // PACK
            for i, piece in enumerate(grouped):
                cols = slice(i * w, (i + 1) * w)
                nc.vector.quantize_mx(out=codes[:, cols].bitcast(FP8X4), scales=scales[:, cols], in_=piece[:])

        def stage_a(e, copy):
            w1_grouped[e] = pieces(1, e)
            nt = 4 // len(w1_grouped[e])
            for i, piece in enumerate(w1_grouped[e]):
                copy(
                    out=piece[:].rearrange("p (t m j) -> p m j t", t=nt, j=PACK),
                    in_=raw_of[(1, e)][:].rearrange("p j (m t) -> p m j t", t=4)[:, :, :, i * nt:(i + 1) * nt],
                )

        def stage_b(e):
            codes = quant.tile([P, H], U32, tag="w1c", align_bytes=64)
            scales = quant.tile([P, H], U8, tag="w1s", align_bytes=64)
            quantise(codes, scales, w1_grouped[e])
            w1_q[e] = (codes, scales)

        def stage_c(e):
            codes, scales = w1_q[e]
            acc = psum1.tile([P, 4, C], F32, tag="ps1")
            for t in range(4):
                nc.tensor.matmul_mx(
                    out=acc[:, t, :],
                    lhsT=codes[:, t * P:(t + 1) * P].bitcast(FP8X4),
                    lhsT_scale=scales[:, t * P:(t + 1) * P],
                    rhs=slot_codes[:, e * C:(e + 1) * C].bitcast(FP8X4),
                    rhs_scale=slot_scales[:, e * C:(e + 1) * C],
                    start=True,
                    stop=True,
                )
            l1_acc[e] = acc

        def stage_d(e):
            h_grouped = quant.tile([P, PACK * C], BF16, tag="hg", align_bytes=64)
            nc.scalar.activation(
                out=h_grouped[:].rearrange("p (c t) -> p c t", t=4),
                in_=l1_acc[e][:].rearrange("p t c -> p c t"),
                func=SILU,
            )
            l1_acc[e] = h_grouped

        def stage_f(e):
            if e in H_TAKES:
                h_codes = shared.tile([P, C], U32, tag=H_TAKES[e], name="h_codes_late", align_bytes=64)
            else:
                h_codes = quant.tile([P, C], U32, tag="hc", name="h_codes", align_bytes=64)
            h_scales = quant.tile([P, C], U8, tag="hs", align_bytes=64)
            nc.vector.quantize_mx(out=h_codes[:].bitcast(FP8X4), scales=h_scales[:], in_=l1_acc[e][:])
            h_q[e] = (h_codes, h_scales)

        def stage_g(e):
            raw = raw_of[(2, e)]
            if (2, e) in HALVED:
                w2_grouped[e] = pieces(2, e)
                w = N // len(w2_grouped[e])
                for i, piece in enumerate(w2_grouped[e]):
                    plain_interleave(nc.vector.tensor_copy, piece, raw[:, :, i * w:(i + 1) * w], 0, w)
                return
            if e == E - 4:
                grouped = shared.tile([P, PACK * N], BF16, tag="g2_4", name="grouped_late", align_bytes=64)
            else:
                grouped = stage.tile([P, PACK * N], BF16, tag="grouped", name="grouped", align_bytes=64)
            split = {E - 4: P, E - 3: 2 * P}.get(e, 0)
            if split > 0:
                plain_interleave(nc.vector.tensor_copy, grouped, raw, 0, split)
            if split < N:
                plain_interleave(nc.scalar.copy, grouped, raw, split, N)
            w2_grouped[e] = [grouped]

        def stage_hq(e):
            if e == E - 4:
                codes = shared.tile([P, N], U32, tag="w1_6", name="codes_late", align_bytes=64)
            else:
                codes = quant.tile([P, N], U32, tag="w2c", name="codes", align_bytes=64)
            scales = quant.tile([P, N], U8, tag="w2s", align_bytes=64)
            quantise(codes, scales, w2_grouped[e])
            w2_q[e] = (codes, scales)

        def stage_l(e, blocks, first=0):
            codes, scales = w2_q[e]
            h_codes, h_scales = h_q[e]
            q = e % GROUP
            for nb in blocks:
                if q == 0:
                    y_acc[nb] = psum2.tile([P, GROUP * C], F32, tag="yb%d" % nb, name="yb%d" % nb)
                nc.tensor.matmul_mx(
                    out=y_acc[nb][:, q * C:(q + 1) * C],
                    lhsT=codes[:, (nb - first) * P:(nb - first + 1) * P].bitcast(FP8X4),
                    lhsT_scale=scales[:, (nb - first) * P:(nb - first + 1) * P],
                    rhs=h_codes[:].bitcast(FP8X4),
                    rhs_scale=h_scales[:],
                    start=True,
                    stop=True,
                )

        def last_half(i, shares):
            e = E - 1
            pieces_of = []
            for copy, a, b in shares:
                piece = stage.tile([P, PACK * (b - a)], BF16, tag="last%d" % (b - a), name="last%d" % (b - a), align_bytes=64)
                plain_interleave(copy, piece, last_halves[i][:, :, a:b], 0, b - a)
                pieces_of.append((piece, a, b))
            if i == 0:
                stage_f(e)
            for piece, a, b in pieces_of:
                codes = quant.tile([P, b - a], U32, tag="last_c%d" % i, name="last_c", align_bytes=64)
                scales = quant.tile([P, b - a], U8, tag="last_s%d" % i, name="last_s", align_bytes=64)
                quantise(codes, scales, [piece])
                w2_q[e] = (codes, scales)
                stage_l(e, range((2 * i * P + a) // P, (2 * i * P + b) // P), (2 * i * P + a) // P)

        def stage_y(e, nb, copy, experts):
            s0 = (e + 1 - experts) * C
            q0 = s0 % (GROUP * C)
            copy(out=y_sb[nb][:, s0:s0 + experts * C], in_=y_acc[nb][:, q0:q0 + experts * C])

        plain_interleave(nc.vector.tensor_copy, x_grouped, x_raw, 0, T // 2)
        plain_interleave(nc.scalar.copy, x_grouped, x_raw, T // 2, T)
        stage_a(0, nc.scalar.copy)
        nc.vector.quantize_mx(out=x_codes[:].bitcast(FP8X4), scales=x_scales[:], in_=x_grouped[:])
        gather(0)
        stage_a(1, nc.vector.tensor_copy)
        stage_b(0)
        stage_c(0)
        stage_d(0)
        gather(1)
        gather(2)

        for e in range(E - 1):
            stage_g(e)
            if e + 2 < E:
                stage_a(e + 2, nc.vector.tensor_copy)
            stage_f(e)
            stage_b(e + 1)
            stage_c(e + 1)
            stage_d(e + 1)
            stage_hq(e)
            stage_l(e, range(NB))
            if e == GROUP - 1:
                for nb in range(NB):
                    stage_y(e, nb, nc.scalar.copy, GROUP)
            if e == E - 3:
                stage_y(e, 0, nc.scalar.copy, 2)
        last_half(0, ((nc.scalar.copy, 0, P), (nc.vector.tensor_copy, P, 2 * P)))
        stage_y(E - 1, 0, nc.scalar.copy, 2)
        stage_y(E - 1, 1, nc.scalar.copy, GROUP)
        last_half(1, ((nc.vector.tensor_copy, 0, P), (nc.vector.tensor_copy, P, 2 * P)))
        for nb in (2, 3):
            stage_y(E - 1, nb, nc.scalar.copy, GROUP)

        half = T // 2
        for nb in range(NB):
            first = comb.tile([P, T], F32, tag="first")
            nc.vector.tensor_tensor(first[:], y_sb[nb][:].indirect(pos1_t[:]), gate_t[nb][:, 0, :], MULT)
            second = comb.tile([P, T], F32, tag="second")
            total = comb.tile([P, T], F32, tag="total")
            for engine, t0, t1 in ((("T", 0, T),), (("T", 0, T),), (("T", 0, half), ("V", half, T)), (("V", 0, half), ("V", half, T)))[nb]:
                nc.vector.tensor_tensor(
                    second[:, t0:t1], y_sb[nb][:].indirect(pos2_t[:, t0 // 16:t1 // 16]), gate_t[nb][:, 1, t0:t1], MULT
                )
                rows = out[nb * P:(nb + 1) * P, t0:t1]
                if engine == "T":
                    acc = psum3.tile([P, T], F32, tag="sum")
                    nc.tensor.matmul(acc[:, t0:t1], ident[:], first[:, t0:t1], start=True, stop=False)
                    nc.tensor.matmul(acc[:, t0:t1], ident[:], second[:, t0:t1], start=False, stop=True)
                    nc.scalar.copy(out=total[:, t0:t1], in_=acc[:, t0:t1])
                    nc.scalar.dma_start(out=rows, in_=total[:, t0:t1])
                else:
                    nc.vector.tensor_tensor(total[:, t0:t1], first[:, t0:t1], second[:, t0:t1], ADD)
                    nc.sync.dma_start(out=rows, in_=total[:, t0:t1])
